import numpy as np
import ml_dtypes


def mxq(x, axis, fmt="e4m3"):
    dtype, down = {"e4m3": (ml_dtypes.float8_e4m3fn, 7), "e5m2": (ml_dtypes.float8_e5m2, 14)}[fmt]
    v = np.moveaxis(np.asarray(x, np.float32).astype(ml_dtypes.bfloat16).astype(np.float64), axis, -1)
    blocks = v.reshape(v.shape[:-1] + (-1, 32))
    amax = np.abs(blocks).max(-1, keepdims=True)
    byte = np.maximum(np.where(amax > 0, np.frexp(amax)[1] - 1 + 127, 0) - down, 1)
    scale = np.exp2(byte - 127.0)
    codes = (blocks / scale).astype(np.float32).astype(dtype).astype(np.float64)
    return np.moveaxis((codes * scale).reshape(v.shape), -1, axis)


WIDE = False


def mx_kscale(k, group=512):
    if not WIDE:
        return np.ones(k)
    levels = np.array([10, -10, 5, -5, 0])
    if group != 512:
        return np.exp2(np.random.permutation(np.resize(levels, k // group))).repeat(group)
    if k % 512:
        return np.exp2(np.random.permutation(np.resize(levels, k // 32))).repeat(32)
    a = np.empty((k // 512, 16))
    for p in range(k // 512):
        a[p, :8] = np.random.permutation(np.resize(levels, 8))
        for g in range(8):
            far = levels[np.abs(levels - a[p, g]) >= 10]
            a[p, g + 8] = far[np.random.randint(len(far))]
    return np.exp2(a.ravel()).repeat(32)


def f64(x):
    return np.asarray(x).astype(np.float64)


def striped(idx):
    return np.tile(np.asarray(idx).reshape(-1, 16).T, (8, 1)).astype(np.uint16)


def unstriped(offs):
    return offs[:16].T.reshape(-1).astype(np.int64)


H, KV, D, NQ, N = 4, 4, 128, 512, 512


def setup_inputs():
    n = np.random.standard_normal
    s = mx_kscale(D, 0)[:, None]
    u = mx_kscale(N)
    t = np.random.uniform(0.5, 2.0, N) * u
    v = n((KV, N, 128))
    return {
        "qT": (n((H, D, NQ)) * s * (0.70 / np.sqrt(D))).astype(np.float32),
        "kT": (n((KV, D, N)) / s).astype(np.float32),
        "t": t.reshape(N, 1).astype(np.float32),
        "v": (v / t[:, None]).astype(np.float32),
        "og": n((H, NQ, 128)).astype(np.float32),
    }


def reference(qT, kT, t, v, og):
    a = mxq(f64(kT), 1, "e4m3").transpose(0, 2, 1) @ mxq(f64(qT), 1, "e4m3")
    p = 1.0 / (1.0 + np.exp(-a))
    w = p * f64(t)
    y = mxq(w, 1, "e4m3").transpose(0, 2, 1) @ mxq(f64(v), 1, "e4m3")
    y = y / 16.0
    y = y / (1.0 + np.exp(-f64(og)))
    return y

@@ -1,0 +1,226 @@
+from contextlib import ExitStack
+
+import concourse.mybir as mybir
+
+H, D, NQ, N, E = 4, 128, 512, 512, 128
+FLOPS = 2 * H * N * NQ * D + 2 * H * NQ * N * E
+
+F32 = mybir.dt.float32
+BF16 = mybir.dt.bfloat16
+U32 = mybir.dt.uint32
+U8 = mybir.dt.uint8
+FP8X4 = mybir.dt.float8_e4m3fn_x4
+SIGMOID = mybir.ActivationFunctionType.Sigmoid
+MULT = mybir.AluOpType.mult
+
+P = 128
+PACK = 4
+ROWS = D // PACK
+QB = 128
+HALF = 256
+UNITS = 16
+K_SPLIT = 40
+
+
+def tile_rows_sigmoid_gate_kernel(tc, qT, kT, t, v, og, out):
+    nc = tc.nc
+    with ExitStack() as ctx:
+        sb = ctx.enter_context(tc.tile_pool(name="sb", bufs=1))
+        ps = ctx.enter_context(tc.psum_pool(name="ps", bufs=1))
+        ctx.enter_context(tc.manual_schedule())
+
+        def tiles(name, count, shape, dtype):
+            return [sb.tile(shape, dtype, name="%s%d" % (name, i), align_bytes=64) for i in range(count)]
+
+        q_raw = tiles("q_raw", 2, [P, PACK, HALF], F32)
+        k_raw = tiles("k_raw", 2, [P, PACK, HALF], F32)
+        v_raw = tiles("v_raw", 2, [P, 2, PACK, E], F32)
+        og_raw = tiles("og_raw", 2, [P, H, 2 * E], F32)
+        t_sb = sb.tile([P, PACK], F32, name="t_sb", align_bytes=64)
+        warm = sb.tile([P, 8], F32, name="warm", align_bytes=64)
+        warm_out = sb.tile([P, 8], F32, name="warm_out", align_bytes=64)
+
+        q_bf = tiles("q_bf", 2, [P, 2 * QB * PACK], BF16)
+        k_bf = tiles("k_bf", 2, [P, PACK * 64 * PACK], BF16)
+        v_bf = tiles("v_bf", H, [P, E * PACK], BF16)
+        q_codes = tiles("q_codes", 2, [P, HALF], U32)
+        q_scales = tiles("q_scales", 2, [P, HALF], U8)
+        k_codes = tiles("k_codes", PACK, [P, P], U32)
+        k_scales = tiles("k_scales", PACK, [P, P], U8)
+        v_codes = tiles("v_codes", H, [P, E], U32)
+        v_scales = tiles("v_scales", H, [P, E], U8)
+        p_sb = tiles("p_sb", UNITS, [P, QB * PACK], F32)
+        w_bf = tiles("w_bf", UNITS, [P, QB * PACK], BF16)
+        w_codes = tiles("w_codes", UNITS, [P, QB], U32)
+        w_scales = tiles("w_scales", UNITS, [P, QB], U8)
+        gate = tiles("gate", 4, [P, 2 * 2 * E], F32)
+        res = tiles("res", 5, [P, 2 * 2 * E], F32)
+        s_bank = [ps.tile([P, PACK * QB], F32, name="s_bank%d" % h) for h in range(H)]
+        y_bank = [ps.tile([P, 2 * 2 * E], F32, name="y_bank%d" % b) for b in range(4)]
+
+        q_rows = qT.rearrange("h (p j) n -> (h p) j n", j=PACK)
+        k_rows = kT.rearrange("h (p j) n -> (h p) j n", j=PACK)
+        v_rows = v.rearrange("h (p j) e -> p h j e", j=PACK)
+
+        def query_rows(x, u):
+            return x[:, u * HALF : (u + 1) * HALF, :].rearrange("h (p x) e -> p h (x e)", x=2)
+
+        nc.scalar.dma_start(out=t_sb[:], in_=t.rearrange("(p j) o -> p (j o)", j=PACK))
+        nc.sync.dma_start(out=q_raw[0][:], in_=q_rows[:, :, 0:HALF])
+        nc.sync.dma_start(out=k_raw[0][:], in_=k_rows[:, :, 0:HALF])
+        nc.sync.dma_start(out=k_raw[1][:], in_=k_rows[:, :, HALF:N])
+        nc.sync.dma_start(out=q_raw[1][:], in_=q_rows[:, :, HALF:NQ])
+        for c in range(2):
+            nc.sync.dma_start(out=v_raw[c][:], in_=v_rows[:, 2 * c : 2 * c + 2, :, :])
+        for u in range(2):
+            nc.sync.dma_start(out=og_raw[u][:], in_=query_rows(og, u))
+
+        nc.gpsimd.memset(warm[:], 0.0)
+        nc.scalar.activation(out=warm_out[:], in_=warm[:], func=SIGMOID)
+
+        def quantize(codes, scales, values):
+            nc.vector.quantize_mx(out=codes.bitcast(FP8X4), scales=scales, in_=values)
+
+        def pack_q(u):
+            nc.vector.tensor_copy(
+                out=q_bf[u][:].rearrange("p (x n j) -> p n x j", x=2, j=PACK),
+                in_=q_raw[u][:].rearrange("p j (n x) -> p n x j", x=2),
+            )
+
+        def pack_k(copy, c, s0, s1):
+            copy(
+                out=k_bf[c][:].rearrange("p (r s j) -> p s r j", r=PACK, j=PACK)[:, s0:s1],
+                in_=k_raw[c][:].rearrange("p j (s r) -> p s r j", r=PACK)[:, s0:s1],
+            )
+
+        def quantize_k(c):
+            for r in range(PACK):
+                window = slice(64 * c, 64 * (c + 1))
+                quantize(k_codes[r][:, window], k_scales[r][:, window], k_bf[c][:, r * HALF : (r + 1) * HALF])
+
+        def pack_v(h):
+            nc.scalar.copy(
+                out=v_bf[h][:].rearrange("p (e j) -> p e j", j=PACK),
+                in_=v_raw[h // 2][:, h % 2].rearrange("p j e -> p e j"),
+            )
+
+        def unit(i):
+            return i // 8, (i // 4) % 2, i % 4
+
+        def scores(i):
+            u, x, h = unit(i)
+            rows = slice(ROWS * h, ROWS * (h + 1))
+            cols = slice(QB * x, QB * (x + 1))
+            for r in range(PACK):
+                nc.tensor.matmul_mx(
+                    out=s_bank[h][:, r * QB : (r + 1) * QB],
+                    lhsT=k_codes[r][rows, :].bitcast(FP8X4),
+                    lhsT_scale=k_scales[r][rows, :],
+                    rhs=q_codes[u][rows, cols].bitcast(FP8X4),
+                    rhs_scale=q_scales[u][rows, cols],
+                    start=True,
+                    stop=True,
+                )
+
+        def sigmoid(i):
+            nc.scalar.activation(
+                out=p_sb[i][:].rearrange("p (n r) -> p n r", r=PACK),
+                in_=s_bank[i % H][:].rearrange("p (r n) -> p n r", r=PACK),
+                func=SIGMOID,
+            )
+
+        def weigh(i):
+            nc.vector.tensor_tensor(
+                out=w_bf[i][:].rearrange("p (n r) -> p n r", r=PACK),
+                in0=p_sb[i][:].rearrange("p (n r) -> p n r", r=PACK),
+                in1=t_sb[:, 0:PACK].unsqueeze(1).to_broadcast([P, QB, PACK]),
+                op=MULT,
+            )
+
+        def quantize_w(i):
+            quantize(w_codes[i][:], w_scales[i][:], w_bf[i][:])
+
+        def y_place(u, h):
+            if (u, h) == (1, 3):
+                return 0, 0
+            return 2 * u + h // 2, (h % 2) * 2 * E
+
+        def values(i):
+            u, x, h = unit(i)
+            b, c0 = y_place(u, h)
+            nc.tensor.matmul_mx(
+                out=y_bank[b][:, c0 + x * E : c0 + (x + 1) * E],
+                lhsT=w_codes[i][:].bitcast(FP8X4),
+                lhsT_scale=w_scales[i][:],
+                rhs=v_codes[h][:].bitcast(FP8X4),
+                rhs_scale=v_scales[h][:],
+                start=True,
+                stop=True,
+            )
+
+        def gates(u, c):
+            nc.scalar.activation(
+                out=gate[2 * u + c][:],
+                in_=og_raw[u][:, 2 * c : 2 * c + 2, :].rearrange("p h f -> p (h f)"),
+                func=SIGMOID,
+            )
+
+        def finish(u, h0, h1, tile):
+            b, c0 = y_place(u, h0)
+            width = (h1 - h0) * 2 * E
+            g0 = (h0 % 2) * 2 * E
+            nc.vector.scalar_tensor_tensor(
+                out=tile[:, 0:width],
+                in0=y_bank[b][:, c0 : c0 + width],
+                scalar=1.0 / 16.0,
+                in1=gate[2 * u + h0 // 2][:, g0 : g0 + width],
+                op0=MULT,
+                op1=MULT,
+            )
+            nc.sync.dma_start(
+                out=query_rows(out, u)[:, h0:h1, :],
+                in_=tile[:, 0:width].rearrange("p (h f) -> p h f", f=2 * E),
+            )
+
+        def quantize_v(h):
+            quantize(v_codes[h][:], v_scales[h][:], v_bf[h][:])
+
+        pack_q(0)
+        pack_k(nc.vector.tensor_copy, 0, 0, 64)
+        quantize(q_codes[0][:], q_scales[0][:], q_bf[0][:])
+        quantize_k(0)
+        pack_k(nc.vector.tensor_copy, 1, 0, K_SPLIT)
+        pack_k(nc.scalar.copy, 1, K_SPLIT, 64)
+        quantize_k(1)
+        for i in range(H):
+            scores(i)
+        pack_q(1)
+
+        pack_v_after = {3: 0, 5: 1, 8: 2, 10: 3}
+        gates_after = {7: (0, 0), 11: (0, 1), 13: (1, 0), 15: (1, 1)}
+        quantize_v_after = {4: 0, 6: 1, 9: 2, 10: 3}
+        values_after = {4: [0], 5: [4], 6: [1, 5], 9: [2, 6, 8], 10: [3, 7, 9], 11: [10], 12: [11], 13: [12], 14: [13], 15: [14]}
+        finish_after = {7: (0, 0, 2, res[0]), 11: (0, 2, 4, res[1]), 15: (1, 0, 2, res[2])}
+        for i in range(UNITS):
+            sigmoid(i)
+            if i in pack_v_after:
+                pack_v(pack_v_after[i])
+            if i in gates_after:
+                gates(*gates_after[i])
+            if i + H < UNITS:
+                scores(i + H)
+            weigh(i)
+            if i == 0:
+                quantize(q_codes[1][:], q_scales[1][:], q_bf[1][:])
+            else:
+                quantize_w(i - 1)
+            if i in quantize_v_after:
+                quantize_v(quantize_v_after[i])
+            for j in values_after.get(i, []):
+                values(j)
+            if i in finish_after:
+                finish(*finish_after[i])
+        quantize_w(UNITS - 1)
+        values(UNITS - 1)
+        finish(1, 2, 3, res[3])
+        finish(1, 3, 4, res[4])

@@ -17,9 +17,10 @@ P = 128
 PACK = 4
 ROWS = D // PACK
 QB = 128
-HALF = 256
-UNITS = 16
-K_SPLIT = 40
+UNIT = QB * PACK
+GROUPS = ((0, 1), (128, 2), (384, 1))
+ROUNDS = ((0, 0), (1, 0), (1, 1), (2, 0))
+K_SPLIT = 88
 
 
 def tile_rows_sigmoid_gate_kernel(tc, qT, kT, t, v, og, out):
@@ -29,198 +30,244 @@ def tile_rows_sigmoid_gate_kernel(tc, qT, kT, t, v, og, out):
         ps = ctx.enter_context(tc.psum_pool(name="ps", bufs=1))
         ctx.enter_context(tc.manual_schedule())
 
-        def tiles(name, count, shape, dtype):
-            return [sb.tile(shape, dtype, name="%s%d" % (name, i), align_bytes=64) for i in range(count)]
+        def tile(name, shape, dtype):
+            return sb.tile(shape, dtype, name=name, align_bytes=64)
 
-        q_raw = tiles("q_raw", 2, [P, PACK, HALF], F32)
-        k_raw = tiles("k_raw", 2, [P, PACK, HALF], F32)
-        v_raw = tiles("v_raw", 2, [P, 2, PACK, E], F32)
-        og_raw = tiles("og_raw", 2, [P, H, 2 * E], F32)
-        t_sb = sb.tile([P, PACK], F32, name="t_sb", align_bytes=64)
-        warm = sb.tile([P, 8], F32, name="warm", align_bytes=64)
-        warm_out = sb.tile([P, 8], F32, name="warm_out", align_bytes=64)
+        def by_group(name, shape, dtype):
+            return [tile("%s%d" % (name, g), shape(m), dtype) for g, (q0, m) in enumerate(GROUPS)]
 
-        q_bf = tiles("q_bf", 2, [P, 2 * QB * PACK], BF16)
-        k_bf = tiles("k_bf", 2, [P, PACK * 64 * PACK], BF16)
-        v_bf = tiles("v_bf", H, [P, E * PACK], BF16)
-        q_codes = tiles("q_codes", 2, [P, HALF], U32)
-        q_scales = tiles("q_scales", 2, [P, HALF], U8)
-        k_codes = tiles("k_codes", PACK, [P, P], U32)
-        k_scales = tiles("k_scales", PACK, [P, P], U8)
-        v_codes = tiles("v_codes", H, [P, E], U32)
-        v_scales = tiles("v_scales", H, [P, E], U8)
-        p_sb = tiles("p_sb", UNITS, [P, QB * PACK], F32)
-        w_bf = tiles("w_bf", UNITS, [P, QB * PACK], BF16)
-        w_codes = tiles("w_codes", UNITS, [P, QB], U32)
-        w_scales = tiles("w_scales", UNITS, [P, QB], U8)
-        gate = tiles("gate", 4, [P, 2 * 2 * E], F32)
-        res = tiles("res", 5, [P, 2 * 2 * E], F32)
-        s_bank = [ps.tile([P, PACK * QB], F32, name="s_bank%d" % h) for h in range(H)]
-        y_bank = [ps.tile([P, 2 * 2 * E], F32, name="y_bank%d" % b) for b in range(4)]
+        def by_index(name, count, shape, dtype):
+            return [tile("%s%d" % (name, i), shape, dtype) for i in range(count)]
+
+        k_raw = tile("k_raw", [P, PACK, N], F32)
+        q_raw = by_group("q_raw", lambda m: [P, PACK, m * QB], F32)
+        v_raw = by_index("v_raw", 2, [P, 2, PACK, E], F32)
+        og_raw = by_group("og_raw", lambda m: [P, H * m * E], F32)
+        t_sb = tile("t_sb", [P, PACK], F32)
+        warm = tile("warm", [P, 8], F32)
+        warm_out = tile("warm_out", [P, 8], F32)
+
+        k_bf = tile("k_bf", [P, N * PACK], BF16)
+        k_codes = tile("k_codes", [P, N], U32)
+        k_scales = tile("k_scales", [P, N], U8)
+        q_bf = by_group("q_bf", lambda m: [P, m * UNIT], BF16)
+        q_codes = by_group("q_codes", lambda m: [P, m * QB], U32)
+        q_scales = by_group("q_scales", lambda m: [P, m * QB], U8)
+        v_bf = tile("v_bf", [P, H * E * PACK], BF16)
+        v_codes = tile("v_codes", [P, H * E], U32)
+        v_scales = tile("v_scales", [P, H * E], U8)
+        p_sb = by_index("p_sb", 4, [P, H * UNIT], F32)
+        w_bf = by_index("w_bf", 4, [P, H * UNIT], BF16)
+        w_codes = by_index("w_codes", 4, [P, H * QB], U32)
+        w_scales = by_index("w_scales", 4, [P, H * QB], U8)
+        gate = by_group("gate", lambda m: [P, H * m * E], F32)
+        res = by_group("res", lambda m: [P, H * m * E], F32)
+        s_bank = [ps.tile([P, UNIT], F32, name="s_bank%d" % h) for h in range(H)]
+        y_bank = [ps.tile([P, 4 * E], F32, name="y_bank%d" % b) for b in range(4)]
 
         q_rows = qT.rearrange("h (p j) n -> (h p) j n", j=PACK)
         k_rows = kT.rearrange("h (p j) n -> (h p) j n", j=PACK)
         v_rows = v.rearrange("h (p j) e -> p h j e", j=PACK)
 
-        def query_rows(x, u):
-            return x[:, u * HALF : (u + 1) * HALF, :].rearrange("h (p x) e -> p h (x e)", x=2)
+        def query_rows(x, g):
+            q0, m = GROUPS[g]
+            return x[:, q0 : q0 + m * QB, :].rearrange("h (p x) e -> p h (x e)", x=m)
 
-        nc.scalar.dma_start(out=t_sb[:], in_=t.rearrange("(p j) o -> p (j o)", j=PACK))
-        nc.sync.dma_start(out=q_raw[0][:], in_=q_rows[:, :, 0:HALF])
-        nc.sync.dma_start(out=k_raw[0][:], in_=k_rows[:, :, 0:HALF])
-        nc.sync.dma_start(out=k_raw[1][:], in_=k_rows[:, :, HALF:N])
-        nc.sync.dma_start(out=q_raw[1][:], in_=q_rows[:, :, HALF:NQ])
+        def load_q(g):
+            q0, m = GROUPS[g]
+            nc.sync.dma_start(out=q_raw[g][:], in_=q_rows[:, :, q0 : q0 + m * QB])
+
+        nc.sync.dma_start(out=k_raw[:], in_=k_rows)
+        load_q(0)
+        load_q(1)
+        nc.sync.dma_start(out=t_sb[:], in_=t.rearrange("(p j) o -> p (j o)", j=PACK))
         for c in range(2):
             nc.sync.dma_start(out=v_raw[c][:], in_=v_rows[:, 2 * c : 2 * c + 2, :, :])
-        for u in range(2):
-            nc.sync.dma_start(out=og_raw[u][:], in_=query_rows(og, u))
+        load_q(2)
+        for g in range(3):
+            nc.sync.dma_start(out=og_raw[g][:].rearrange("p (h f) -> p h f", h=H), in_=query_rows(og, g))
 
         nc.gpsimd.memset(warm[:], 0.0)
         nc.scalar.activation(out=warm_out[:], in_=warm[:], func=SIGMOID)
 
-        def quantize(codes, scales, values):
-            nc.vector.quantize_mx(out=codes.bitcast(FP8X4), scales=scales, in_=values)
-
-        def pack_q(u):
-            nc.vector.tensor_copy(
-                out=q_bf[u][:].rearrange("p (x n j) -> p n x j", x=2, j=PACK),
-                in_=q_raw[u][:].rearrange("p j (n x) -> p n x j", x=2),
+        def quantize(codes, scales, values, w0, w1):
+            nc.vector.quantize_mx(
+                out=codes[:, w0:w1].bitcast(FP8X4), scales=scales[:, w0:w1], in_=values[:, PACK * w0 : PACK * w1]
             )
 
-        def pack_k(copy, c, s0, s1):
+        def pack_q(copy, g):
+            m = GROUPS[g][1]
             copy(
-                out=k_bf[c][:].rearrange("p (r s j) -> p s r j", r=PACK, j=PACK)[:, s0:s1],
-                in_=k_raw[c][:].rearrange("p j (s r) -> p s r j", r=PACK)[:, s0:s1],
+                out=q_bf[g][:].rearrange("p (x n j) -> p n x j", x=m, j=PACK),
+                in_=q_raw[g][:].rearrange("p j (n x) -> p n x j", x=m),
             )
 
-        def quantize_k(c):
-            for r in range(PACK):
-                window = slice(64 * c, 64 * (c + 1))
-                quantize(k_codes[r][:, window], k_scales[r][:, window], k_bf[c][:, r * HALF : (r + 1) * HALF])
+        def quantize_q(g):
+            quantize(q_codes[g], q_scales[g], q_bf[g], 0, GROUPS[g][1] * QB)
 
-        def pack_v(h):
-            nc.scalar.copy(
-                out=v_bf[h][:].rearrange("p (e j) -> p e j", j=PACK),
+        def pack_k(copy, s0, s1):
+            copy(
+                out=k_bf[:].rearrange("p (r s j) -> p s r j", r=PACK, j=PACK)[:, s0:s1],
+                in_=k_raw[:].rearrange("p j (s r) -> p s r j", r=PACK)[:, s0:s1],
+            )
+
+        def pack_v(copy, h):
+            copy(
+                out=v_bf[:, h * UNIT : (h + 1) * UNIT].rearrange("p (e j) -> p e j", j=PACK),
                 in_=v_raw[h // 2][:, h % 2].rearrange("p j e -> p e j"),
             )
 
-        def unit(i):
-            return i // 8, (i // 4) % 2, i % 4
+        def quantize_v(h0, h1):
+            quantize(v_codes, v_scales, v_bf, h0 * E, h1 * E)
 
-        def scores(i):
-            u, x, h = unit(i)
-            rows = slice(ROWS * h, ROWS * (h + 1))
+        def scores(n, h0):
+            g, x = ROUNDS[n]
             cols = slice(QB * x, QB * (x + 1))
             for r in range(PACK):
+                tokens = slice(r * P, (r + 1) * P)
+                for h in (h0, h0 + 1):
+                    rows = slice(ROWS * h, ROWS * (h + 1))
+                    nc.tensor.matmul_mx(
+                        out=s_bank[h][:, r * QB : (r + 1) * QB],
+                        lhsT=k_codes[rows, tokens].bitcast(FP8X4),
+                        lhsT_scale=k_scales[rows, tokens],
+                        rhs=q_codes[g][rows, cols].bitcast(FP8X4),
+                        rhs_scale=q_scales[g][rows, cols],
+                        start=True,
+                        stop=True,
+                    )
+
+        def sigmoid(n, h):
+            nc.scalar.activation(
+                out=p_sb[n][:, h * UNIT : (h + 1) * UNIT].rearrange("p (n r) -> p n r", r=PACK),
+                in_=s_bank[h][:].rearrange("p (r n) -> p n r", r=PACK),
+                func=SIGMOID,
+            )
+
+        def weigh(n, h0, h1):
+            cols = slice(h0 * UNIT, h1 * UNIT)
+            nc.vector.tensor_tensor(
+                out=w_bf[n][:, cols].rearrange("p (n r) -> p n r", r=PACK),
+                in0=p_sb[n][:, cols].rearrange("p (n r) -> p n r", r=PACK),
+                in1=t_sb[:, 0:PACK].unsqueeze(1).to_broadcast([P, (h1 - h0) * QB, PACK]),
+                op=MULT,
+            )
+
+        def quantize_w(n, h0, h1):
+            quantize(w_codes[n], w_scales[n], w_bf[n], h0 * QB, h1 * QB)
+
+        def y_place(n, h):
+            if n == 0:
+                return 0, h * E
+            if n < 3:
+                return 1 + h // 2, ((h % 2) * 2 + n - 1) * E
+            return (3 if h < 2 else 0), (h % 2) * E
+
+        def values(n, h0, h1):
+            for h in range(h0, h1):
+                b, c0 = y_place(n, h)
                 nc.tensor.matmul_mx(
-                    out=s_bank[h][:, r * QB : (r + 1) * QB],
-                    lhsT=k_codes[r][rows, :].bitcast(FP8X4),
-                    lhsT_scale=k_scales[r][rows, :],
-                    rhs=q_codes[u][rows, cols].bitcast(FP8X4),
-                    rhs_scale=q_scales[u][rows, cols],
+                    out=y_bank[b][:, c0 : c0 + E],
+                    lhsT=w_codes[n][:, h * QB : (h + 1) * QB].bitcast(FP8X4),
+                    lhsT_scale=w_scales[n][:, h * QB : (h + 1) * QB],
+                    rhs=v_codes[:, h * E : (h + 1) * E].bitcast(FP8X4),
+                    rhs_scale=v_scales[:, h * E : (h + 1) * E],
                     start=True,
                     stop=True,
                 )
 
-        def sigmoid(i):
-            nc.scalar.activation(
-                out=p_sb[i][:].rearrange("p (n r) -> p n r", r=PACK),
-                in_=s_bank[i % H][:].rearrange("p (r n) -> p n r", r=PACK),
-                func=SIGMOID,
-            )
+        def gates(g):
+            nc.scalar.activation(out=gate[g][:], in_=og_raw[g][:], func=SIGMOID)
 
-        def weigh(i):
-            nc.vector.tensor_tensor(
-                out=w_bf[i][:].rearrange("p (n r) -> p n r", r=PACK),
-                in0=p_sb[i][:].rearrange("p (n r) -> p n r", r=PACK),
-                in1=t_sb[:, 0:PACK].unsqueeze(1).to_broadcast([P, QB, PACK]),
-                op=MULT,
-            )
-
-        def quantize_w(i):
-            quantize(w_codes[i][:], w_scales[i][:], w_bf[i][:])
-
-        def y_place(u, h):
-            if (u, h) == (1, 3):
-                return 0, 0
-            return 2 * u + h // 2, (h % 2) * 2 * E
-
-        def values(i):
-            u, x, h = unit(i)
-            b, c0 = y_place(u, h)
-            nc.tensor.matmul_mx(
-                out=y_bank[b][:, c0 + x * E : c0 + (x + 1) * E],
-                lhsT=w_codes[i][:].bitcast(FP8X4),
-                lhsT_scale=w_scales[i][:],
-                rhs=v_codes[h][:].bitcast(FP8X4),
-                rhs_scale=v_scales[h][:],
-                start=True,
-                stop=True,
-            )
-
-        def gates(u, c):
-            nc.scalar.activation(
-                out=gate[2 * u + c][:],
-                in_=og_raw[u][:, 2 * c : 2 * c + 2, :].rearrange("p h f -> p (h f)"),
-                func=SIGMOID,
-            )
-
-        def finish(u, h0, h1, tile):
-            b, c0 = y_place(u, h0)
-            width = (h1 - h0) * 2 * E
-            g0 = (h0 % 2) * 2 * E
+        def finish(g, h0, h1):
+            m = GROUPS[g][1]
+            b, c0 = y_place(ROUNDS.index((g, 0)), h0)
+            cols = slice(h0 * m * E, h1 * m * E)
             nc.vector.scalar_tensor_tensor(
-                out=tile[:, 0:width],
-                in0=y_bank[b][:, c0 : c0 + width],
+                out=res[g][:, cols],
+                in0=y_bank[b][:, c0 : c0 + (h1 - h0) * m * E],
                 scalar=1.0 / 16.0,
-                in1=gate[2 * u + h0 // 2][:, g0 : g0 + width],
+                in1=gate[g][:, cols],
                 op0=MULT,
                 op1=MULT,
             )
             nc.sync.dma_start(
-                out=query_rows(out, u)[:, h0:h1, :],
-                in_=tile[:, 0:width].rearrange("p (h f) -> p h f", f=2 * E),
+                out=query_rows(out, g)[:, h0:h1, :],
+                in_=res[g][:, cols].rearrange("p (h f) -> p h f", f=m * E),
             )
 
-        def quantize_v(h):
-            quantize(v_codes[h][:], v_scales[h][:], v_bf[h][:])
+        vcopy, scopy = nc.vector.tensor_copy, nc.scalar.copy
+        pack_k(vcopy, 0, K_SPLIT)
+        pack_k(scopy, K_SPLIT, P)
+        pack_q(scopy, 0)
+        quantize(k_codes, k_scales, k_bf, 0, N)
+        quantize_q(0)
+        scores(0, 0)
+        scores(0, 2)
+        pack_q(vcopy, 1)
+        quantize_q(1)
+        pack_v(vcopy, 0)
 
-        pack_q(0)
-        pack_k(nc.vector.tensor_copy, 0, 0, 64)
-        quantize(q_codes[0][:], q_scales[0][:], q_bf[0][:])
-        quantize_k(0)
-        pack_k(nc.vector.tensor_copy, 1, 0, K_SPLIT)
-        pack_k(nc.scalar.copy, 1, K_SPLIT, 64)
-        quantize_k(1)
-        for i in range(H):
-            scores(i)
-        pack_q(1)
-
-        pack_v_after = {3: 0, 5: 1, 8: 2, 10: 3}
-        gates_after = {7: (0, 0), 11: (0, 1), 13: (1, 0), 15: (1, 1)}
-        quantize_v_after = {4: 0, 6: 1, 9: 2, 10: 3}
-        values_after = {4: [0], 5: [4], 6: [1, 5], 9: [2, 6, 8], 10: [3, 7, 9], 11: [10], 12: [11], 13: [12], 14: [13], 15: [14]}
-        finish_after = {7: (0, 0, 2, res[0]), 11: (0, 2, 4, res[1]), 15: (1, 0, 2, res[2])}
-        for i in range(UNITS):
-            sigmoid(i)
-            if i in pack_v_after:
-                pack_v(pack_v_after[i])
-            if i in gates_after:
-                gates(*gates_after[i])
-            if i + H < UNITS:
-                scores(i + H)
-            weigh(i)
-            if i == 0:
-                quantize(q_codes[1][:], q_scales[1][:], q_bf[1][:])
-            else:
-                quantize_w(i - 1)
-            if i in quantize_v_after:
-                quantize_v(quantize_v_after[i])
-            for j in values_after.get(i, []):
-                values(j)
-            if i in finish_after:
-                finish(*finish_after[i])
-        quantize_w(UNITS - 1)
-        values(UNITS - 1)
-        finish(1, 2, 3, res[3])
-        finish(1, 3, 4, res[4])
+        sigmoid(0, 0)
+        weigh(0, 0, 1)
+        sigmoid(0, 1)
+        scores(1, 0)
+        weigh(0, 1, 2)
+        sigmoid(0, 2)
+        weigh(0, 2, 3)
+        sigmoid(0, 3)
+        scores(1, 2)
+        quantize_w(0, 0, 2)
+        weigh(0, 3, 4)
+        sigmoid(1, 0)
+        sigmoid(1, 1)
+        scores(2, 0)
+        pack_v(scopy, 1)
+        pack_q(vcopy, 2)
+        quantize_w(0, 2, 4)
+        weigh(1, 0, 2)
+        sigmoid(1, 2)
+        sigmoid(1, 3)
+        scores(2, 2)
+        pack_v(scopy, 2)
+        quantize_q(2)
+        quantize_w(1, 0, 2)
+        weigh(1, 2, 4)
+        sigmoid(2, 0)
+        sigmoid(2, 1)
+        scores(3, 0)
+        pack_v(scopy, 3)
+        quantize_v(0, 2)
+        quantize_w(1, 2, 4)
+        values(0, 0, 2)
+        values(1, 0, 2)
+        weigh(2, 0, 2)
+        sigmoid(2, 2)
+        sigmoid(2, 3)
+        scores(3, 2)
+        gates(0)
+        quantize_v(2, 4)
+        values(0, 2, 4)
+        values(1, 2, 4)
+        quantize_w(2, 0, 2)
+        values(2, 0, 2)
+        weigh(2, 2, 4)
+        sigmoid(3, 0)
+        sigmoid(3, 1)
+        gates(1)
+        finish(0, 0, 4)
+        quantize_w(2, 2, 4)
+        values(2, 2, 4)
+        weigh(3, 0, 2)
+        sigmoid(3, 2)
+        sigmoid(3, 3)
+        gates(2)
+        finish(1, 0, 2)
+        quantize_w(3, 0, 2)
+        values(3, 0, 2)
+        weigh(3, 2, 4)
+        finish(2, 0, 2)
+        quantize_w(3, 2, 4)
+        values(3, 2, 4)
+        finish(1, 2, 4)
+        finish(2, 2, 4)

@@ -21,6 +21,10 @@ UNIT = QB * PACK
 GROUPS = ((0, 1), (128, 2), (384, 1))
 ROUNDS = ((0, 0), (1, 0), (1, 1), (2, 0))
 K_SPLIT = 88
+Q_SPLIT = 40
+LINE = 4
+V_LOADS = ((0, 1), (1, 2), (2, 4))
+Y_LAST = ((3, 0), (3, E), (0, 0), (0, E))
 
 
 def tile_rows_sigmoid_gate_kernel(tc, qT, kT, t, v, og, out):
@@ -41,7 +45,7 @@ def tile_rows_sigmoid_gate_kernel(tc, qT, kT, t, v, og, out):
 
         k_raw = tile("k_raw", [P, PACK, N], F32)
         q_raw = by_group("q_raw", lambda m: [P, PACK, m * QB], F32)
-        v_raw = by_index("v_raw", 2, [P, 2, PACK, E], F32)
+        v_raw = [tile("v_raw%d" % h0, [P, h1 - h0, PACK, E], F32) for h0, h1 in V_LOADS]
         og_raw = by_group("og_raw", lambda m: [P, H * m * E], F32)
         t_sb = tile("t_sb", [P, PACK], F32)
         warm = tile("warm", [P, 8], F32)
@@ -77,15 +81,23 @@ def tile_rows_sigmoid_gate_kernel(tc, qT, kT, t, v, og, out):
             q0, m = GROUPS[g]
             nc.sync.dma_start(out=q_raw[g][:], in_=q_rows[:, :, q0 : q0 + m * QB])
 
+        def load_v(c):
+            nc.sync.dma_start(out=v_raw[c][:], in_=v_rows[:, V_LOADS[c][0] : V_LOADS[c][1], :, :])
+
+        def load_og(g):
+            nc.sync.dma_start(out=og_raw[g][:].rearrange("p (h f) -> p h f", h=H), in_=query_rows(og, g))
+
         nc.sync.dma_start(out=k_raw[:], in_=k_rows)
         load_q(0)
         load_q(1)
+        load_v(0)
         nc.sync.dma_start(out=t_sb[:], in_=t.rearrange("(p j) o -> p (j o)", j=PACK))
-        for c in range(2):
-            nc.sync.dma_start(out=v_raw[c][:], in_=v_rows[:, 2 * c : 2 * c + 2, :, :])
+        load_v(1)
         load_q(2)
-        for g in range(3):
-            nc.sync.dma_start(out=og_raw[g][:].rearrange("p (h f) -> p h f", h=H), in_=query_rows(og, g))
+        load_v(2)
+        load_og(0)
+        load_og(1)
+        load_og(2)
 
         nc.gpsimd.memset(warm[:], 0.0)
         nc.scalar.activation(out=warm_out[:], in_=warm[:], func=SIGMOID)
@@ -95,11 +107,11 @@ def tile_rows_sigmoid_gate_kernel(tc, qT, kT, t, v, og, out):
                 out=codes[:, w0:w1].bitcast(FP8X4), scales=scales[:, w0:w1], in_=values[:, PACK * w0 : PACK * w1]
             )
 
-        def pack_q(copy, g):
+        def pack_q(copy, g, c0=0, c1=None):
             m = GROUPS[g][1]
             copy(
-                out=q_bf[g][:].rearrange("p (x n j) -> p n x j", x=m, j=PACK),
-                in_=q_raw[g][:].rearrange("p j (n x) -> p n x j", x=m),
+                out=q_bf[g][:].rearrange("p (x c i j) -> p c j i x", x=m, i=LINE // m, j=PACK)[:, c0:c1],
+                in_=q_raw[g][:].rearrange("p j (c i x) -> p c j i x", x=m, i=LINE // m)[:, c0:c1],
             )
 
         def quantize_q(g):
@@ -113,8 +125,8 @@ def tile_rows_sigmoid_gate_kernel(tc, qT, kT, t, v, og, out):
 
         def pack_v(copy, h):
             copy(
-                out=v_bf[:, h * UNIT : (h + 1) * UNIT].rearrange("p (e j) -> p e j", j=PACK),
-                in_=v_raw[h // 2][:, h % 2].rearrange("p j e -> p e j"),
+                out=v_bf[:, h * UNIT : (h + 1) * UNIT].rearrange("p (c i j) -> p c j i", i=LINE, j=PACK),
+                in_=v_raw[min(h, 2)][:, max(h - 2, 0)].rearrange("p j (c i) -> p c j i", i=LINE),
             )
 
         def quantize_v(h0, h1):
@@ -161,7 +173,7 @@ def tile_rows_sigmoid_gate_kernel(tc, qT, kT, t, v, og, out):
                 return 0, h * E
             if n < 3:
                 return 1 + h // 2, ((h % 2) * 2 + n - 1) * E
-            return (3 if h < 2 else 0), (h % 2) * E
+            return Y_LAST[h]
 
         def values(n, h0, h1):
             for h in range(h0, h1):
@@ -176,8 +188,9 @@ def tile_rows_sigmoid_gate_kernel(tc, qT, kT, t, v, og, out):
                     stop=True,
                 )
 
-        def gates(g):
-            nc.scalar.activation(out=gate[g][:], in_=og_raw[g][:], func=SIGMOID)
+        def gates(g, h0, h1):
+            cols = slice(h0 * GROUPS[g][1] * E, h1 * GROUPS[g][1] * E)
+            nc.scalar.activation(out=gate[g][:, cols], in_=og_raw[g][:, cols], func=SIGMOID)
 
         def finish(g, h0, h1):
             m = GROUPS[g][1]
@@ -204,10 +217,12 @@ def tile_rows_sigmoid_gate_kernel(tc, qT, kT, t, v, og, out):
         quantize_q(0)
         scores(0, 0)
         scores(0, 2)
-        pack_q(vcopy, 1)
-        quantize_q(1)
-        pack_v(vcopy, 0)
 
+        pack_q(vcopy, 1, 0, Q_SPLIT)
+        pack_q(scopy, 1, Q_SPLIT)
+        pack_v(vcopy, 0)
+        quantize_q(1)
+        pack_v(vcopy, 1)
         sigmoid(0, 0)
         weigh(0, 0, 1)
         sigmoid(0, 1)
@@ -217,54 +232,53 @@ def tile_rows_sigmoid_gate_kernel(tc, qT, kT, t, v, og, out):
         weigh(0, 2, 3)
         sigmoid(0, 3)
         scores(1, 2)
-        quantize_w(0, 0, 2)
         weigh(0, 3, 4)
         sigmoid(1, 0)
         sigmoid(1, 1)
         scores(2, 0)
-        pack_v(scopy, 1)
-        pack_q(vcopy, 2)
-        quantize_w(0, 2, 4)
+        pack_q(scopy, 2)
+        quantize_v(0, 2)
+        quantize_w(0, 0, 4)
+        values(0, 0, 2)
         weigh(1, 0, 2)
         sigmoid(1, 2)
         sigmoid(1, 3)
         scores(2, 2)
-        pack_v(scopy, 2)
         quantize_q(2)
         quantize_w(1, 0, 2)
+        values(1, 0, 2)
         weigh(1, 2, 4)
         sigmoid(2, 0)
         sigmoid(2, 1)
         scores(3, 0)
-        pack_v(scopy, 3)
-        quantize_v(0, 2)
-        quantize_w(1, 2, 4)
-        values(0, 0, 2)
-        values(1, 0, 2)
+        pack_v(scopy, 2)
         weigh(2, 0, 2)
+        quantize_w(1, 2, 4)
         sigmoid(2, 2)
         sigmoid(2, 3)
         scores(3, 2)
-        gates(0)
-        quantize_v(2, 4)
-        values(0, 2, 4)
-        values(1, 2, 4)
+        pack_v(scopy, 3)
         quantize_w(2, 0, 2)
         values(2, 0, 2)
         weigh(2, 2, 4)
         sigmoid(3, 0)
         sigmoid(3, 1)
-        gates(1)
-        finish(0, 0, 4)
+        gates(1, 0, 2)
+        gates(0, 0, 4)
+        quantize_v(2, 4)
+        values(0, 2, 4)
+        values(1, 2, 4)
         quantize_w(2, 2, 4)
         values(2, 2, 4)
         weigh(3, 0, 2)
         sigmoid(3, 2)
         sigmoid(3, 3)
-        gates(2)
+        gates(2, 0, 4)
+        gates(1, 2, 4)
         finish(1, 0, 2)
         quantize_w(3, 0, 2)
         values(3, 0, 2)
+        finish(0, 0, 4)
         weigh(3, 2, 4)
         finish(2, 0, 2)
         quantize_w(3, 2, 4)

@@ -18,13 +18,13 @@ PACK = 4
 ROWS = D // PACK
 QB = 128
 UNIT = QB * PACK
-GROUPS = ((0, 1), (128, 2), (384, 1))
-ROUNDS = ((0, 0), (1, 0), (1, 1), (2, 0))
-K_SPLIT = 88
-Q_SPLIT = 40
 LINE = 4
+
+GROUPS = ((0, 1), (128, 2), (384, 1))
+ROUNDS = tuple((g, x) for g, (q0, m) in enumerate(GROUPS) for x in range(m))
 V_LOADS = ((0, 1), (1, 2), (2, 4))
-Y_LAST = ((3, 0), (3, E), (0, 0), (0, E))
+K_SPLIT = 56
+Q_SPLIT = 40
 
 
 def tile_rows_sigmoid_gate_kernel(tc, qT, kT, t, v, og, out):
@@ -40,15 +40,15 @@ def tile_rows_sigmoid_gate_kernel(tc, qT, kT, t, v, og, out):
         def by_group(name, shape, dtype):
             return [tile("%s%d" % (name, g), shape(m), dtype) for g, (q0, m) in enumerate(GROUPS)]
 
-        def by_index(name, count, shape, dtype):
-            return [tile("%s%d" % (name, i), shape, dtype) for i in range(count)]
+        def by_round(name, shape, dtype):
+            return [tile("%s%d" % (name, n), shape, dtype) for n in range(len(ROUNDS))]
 
         k_raw = tile("k_raw", [P, PACK, N], F32)
         q_raw = by_group("q_raw", lambda m: [P, PACK, m * QB], F32)
         v_raw = [tile("v_raw%d" % h0, [P, h1 - h0, PACK, E], F32) for h0, h1 in V_LOADS]
         og_raw = by_group("og_raw", lambda m: [P, H * m * E], F32)
         t_sb = tile("t_sb", [P, PACK], F32)
-        warm = tile("warm", [P, 8], F32)
+        warm_in = tile("warm_in", [P, 8], F32)
         warm_out = tile("warm_out", [P, 8], F32)
 
         k_bf = tile("k_bf", [P, N * PACK], BF16)
@@ -60,10 +60,10 @@ def tile_rows_sigmoid_gate_kernel(tc, qT, kT, t, v, og, out):
         v_bf = tile("v_bf", [P, H * E * PACK], BF16)
         v_codes = tile("v_codes", [P, H * E], U32)
         v_scales = tile("v_scales", [P, H * E], U8)
-        p_sb = by_index("p_sb", 4, [P, H * UNIT], F32)
-        w_bf = by_index("w_bf", 4, [P, H * UNIT], BF16)
-        w_codes = by_index("w_codes", 4, [P, H * QB], U32)
-        w_scales = by_index("w_scales", 4, [P, H * QB], U8)
+        p_sb = by_round("p_sb", [P, H * UNIT], F32)
+        w_bf = by_round("w_bf", [P, H * UNIT], BF16)
+        w_codes = by_round("w_codes", [P, H * QB], U32)
+        w_scales = by_round("w_scales", [P, H * QB], U8)
         gate = by_group("gate", lambda m: [P, H * m * E], F32)
         res = by_group("res", lambda m: [P, H * m * E], F32)
         s_bank = [ps.tile([P, UNIT], F32, name="s_bank%d" % h) for h in range(H)]
@@ -82,10 +82,8 @@ def tile_rows_sigmoid_gate_kernel(tc, qT, kT, t, v, og, out):
             nc.sync.dma_start(out=q_raw[g][:], in_=q_rows[:, :, q0 : q0 + m * QB])
 
         def load_v(c):
-            nc.sync.dma_start(out=v_raw[c][:], in_=v_rows[:, V_LOADS[c][0] : V_LOADS[c][1], :, :])
-
-        def load_og(g):
-            nc.sync.dma_start(out=og_raw[g][:].rearrange("p (h f) -> p h f", h=H), in_=query_rows(og, g))
+            h0, h1 = V_LOADS[c]
+            nc.sync.dma_start(out=v_raw[c][:], in_=v_rows[:, h0:h1, :, :])
 
         nc.sync.dma_start(out=k_raw[:], in_=k_rows)
         load_q(0)
@@ -95,16 +93,21 @@ def tile_rows_sigmoid_gate_kernel(tc, qT, kT, t, v, og, out):
         load_v(1)
         load_q(2)
         load_v(2)
-        load_og(0)
-        load_og(1)
-        load_og(2)
+        for g in range(len(GROUPS)):
+            nc.sync.dma_start(out=og_raw[g][:].rearrange("p (h f) -> p h f", h=H), in_=query_rows(og, g))
 
-        nc.gpsimd.memset(warm[:], 0.0)
-        nc.scalar.activation(out=warm_out[:], in_=warm[:], func=SIGMOID)
+        nc.gpsimd.memset(warm_in[:], 0.0)
+        nc.scalar.activation(out=warm_out[:], in_=warm_in[:], func=SIGMOID)
 
         def quantize(codes, scales, values, w0, w1):
             nc.vector.quantize_mx(
                 out=codes[:, w0:w1].bitcast(FP8X4), scales=scales[:, w0:w1], in_=values[:, PACK * w0 : PACK * w1]
+            )
+
+        def pack_k(copy, r0, s0, s1):
+            copy(
+                out=k_bf[:].rearrange("p (r s j) -> p s j r", r=PACK, j=PACK)[:, s0:s1, :, r0 : r0 + 2],
+                in_=k_raw[:].rearrange("p j (s r) -> p s j r", r=PACK)[:, s0:s1, :, r0 : r0 + 2],
             )
 
         def pack_q(copy, g, c0=0, c1=None):
@@ -114,53 +117,51 @@ def tile_rows_sigmoid_gate_kernel(tc, qT, kT, t, v, og, out):
                 in_=q_raw[g][:].rearrange("p j (c i x) -> p c j i x", x=m, i=LINE // m)[:, c0:c1],
             )
 
-        def quantize_q(g):
-            quantize(q_codes[g], q_scales[g], q_bf[g], 0, GROUPS[g][1] * QB)
-
-        def pack_k(copy, s0, s1):
-            copy(
-                out=k_bf[:].rearrange("p (r s j) -> p s r j", r=PACK, j=PACK)[:, s0:s1],
-                in_=k_raw[:].rearrange("p j (s r) -> p s r j", r=PACK)[:, s0:s1],
-            )
-
         def pack_v(copy, h):
+            c = min(h, len(V_LOADS) - 1)
             copy(
                 out=v_bf[:, h * UNIT : (h + 1) * UNIT].rearrange("p (c i j) -> p c j i", i=LINE, j=PACK),
-                in_=v_raw[min(h, 2)][:, max(h - 2, 0)].rearrange("p j (c i) -> p c j i", i=LINE),
+                in_=v_raw[c][:, h - V_LOADS[c][0]].rearrange("p j (c i) -> p c j i", i=LINE),
             )
+
+        def quantize_q(g):
+            quantize(q_codes[g], q_scales[g], q_bf[g], 0, GROUPS[g][1] * QB)
 
         def quantize_v(h0, h1):
             quantize(v_codes, v_scales, v_bf, h0 * E, h1 * E)
 
         def scores(n, h0):
             g, x = ROUNDS[n]
-            cols = slice(QB * x, QB * (x + 1))
+            queries = slice(QB * x, QB * (x + 1))
             for r in range(PACK):
                 tokens = slice(r * P, (r + 1) * P)
-                for h in (h0, h0 + 1):
+                for h in (h0 + 1, h0):
                     rows = slice(ROWS * h, ROWS * (h + 1))
                     nc.tensor.matmul_mx(
                         out=s_bank[h][:, r * QB : (r + 1) * QB],
                         lhsT=k_codes[rows, tokens].bitcast(FP8X4),
                         lhsT_scale=k_scales[rows, tokens],
-                        rhs=q_codes[g][rows, cols].bitcast(FP8X4),
-                        rhs_scale=q_scales[g][rows, cols],
+                        rhs=q_codes[g][rows, queries].bitcast(FP8X4),
+                        rhs_scale=q_scales[g][rows, queries],
                         start=True,
                         stop=True,
                     )
 
-        def sigmoid(n, h):
-            nc.scalar.activation(
-                out=p_sb[n][:, h * UNIT : (h + 1) * UNIT].rearrange("p (n r) -> p n r", r=PACK),
-                in_=s_bank[h][:].rearrange("p (r n) -> p n r", r=PACK),
-                func=SIGMOID,
-            )
+        def sigmoids(n, h0):
+            for h in (h0, h0 + 1):
+                nc.scalar.activation(
+                    out=p_sb[n][:, h * UNIT : (h + 1) * UNIT].rearrange("p (q r) -> p q r", r=PACK),
+                    in_=s_bank[h][:].rearrange("p (r q) -> p q r", r=PACK),
+                    func=SIGMOID,
+                )
+            if n + 1 < len(ROUNDS):
+                scores(n + 1, h0)
 
         def weigh(n, h0, h1):
             cols = slice(h0 * UNIT, h1 * UNIT)
             nc.vector.tensor_tensor(
-                out=w_bf[n][:, cols].rearrange("p (n r) -> p n r", r=PACK),
-                in0=p_sb[n][:, cols].rearrange("p (n r) -> p n r", r=PACK),
+                out=w_bf[n][:, cols].rearrange("p (q r) -> p q r", r=PACK),
+                in0=p_sb[n][:, cols].rearrange("p (q r) -> p q r", r=PACK),
                 in1=t_sb[:, 0:PACK].unsqueeze(1).to_broadcast([P, (h1 - h0) * QB, PACK]),
                 op=MULT,
             )
@@ -169,11 +170,12 @@ def tile_rows_sigmoid_gate_kernel(tc, qT, kT, t, v, og, out):
             quantize(w_codes[n], w_scales[n], w_bf[n], h0 * QB, h1 * QB)
 
         def y_place(n, h):
-            if n == 0:
+            g, x = ROUNDS[n]
+            if g == 0:
                 return 0, h * E
-            if n < 3:
-                return 1 + h // 2, ((h % 2) * 2 + n - 1) * E
-            return Y_LAST[h]
+            if g == 1:
+                return 1 + h // 2, ((h % 2) * 2 + x) * E
+            return (3 if h < 2 else 0), (h % 2) * E
 
         def values(n, h0, h1):
             for h in range(h0, h1):
@@ -209,79 +211,68 @@ def tile_rows_sigmoid_gate_kernel(tc, qT, kT, t, v, og, out):
                 in_=res[g][:, cols].rearrange("p (h f) -> p h f", f=m * E),
             )
 
-        vcopy, scopy = nc.vector.tensor_copy, nc.scalar.copy
-        pack_k(vcopy, 0, K_SPLIT)
-        pack_k(scopy, K_SPLIT, P)
-        pack_q(scopy, 0)
-        quantize(k_codes, k_scales, k_bf, 0, N)
+        on_vector, on_scalar = nc.vector.tensor_copy, nc.scalar.copy
+
+        pack_k(on_vector, 0, 0, P)
+        pack_k(on_vector, 2, 0, K_SPLIT)
+        pack_k(on_scalar, 2, K_SPLIT, P)
+        pack_q(on_scalar, 0)
+        quantize(k_codes, k_scales, k_bf, 0, N // 2)
+        quantize(k_codes, k_scales, k_bf, N // 2, N)
         quantize_q(0)
         scores(0, 0)
         scores(0, 2)
-
-        pack_q(vcopy, 1, 0, Q_SPLIT)
-        pack_q(scopy, 1, Q_SPLIT)
-        pack_v(vcopy, 0)
+        pack_q(on_vector, 1, 0, Q_SPLIT)
+        pack_q(on_scalar, 1, Q_SPLIT)
+        pack_v(on_vector, 0)
         quantize_q(1)
-        pack_v(vcopy, 1)
-        sigmoid(0, 0)
-        weigh(0, 0, 1)
-        sigmoid(0, 1)
-        scores(1, 0)
-        weigh(0, 1, 2)
-        sigmoid(0, 2)
-        weigh(0, 2, 3)
-        sigmoid(0, 3)
-        scores(1, 2)
-        weigh(0, 3, 4)
-        sigmoid(1, 0)
-        sigmoid(1, 1)
-        scores(2, 0)
-        pack_q(scopy, 2)
+        pack_v(on_vector, 1)
+
+
+        for h0 in (0, 2):
+            sigmoids(0, h0)
+            weigh(0, h0, h0 + 1)
+            weigh(0, h0 + 1, h0 + 2)
+
+        sigmoids(1, 0)
+        pack_q(on_scalar, 2)
         quantize_v(0, 2)
-        quantize_w(0, 0, 4)
-        values(0, 0, 2)
+        quantize_w(0, 0, H)
         weigh(1, 0, 2)
-        sigmoid(1, 2)
-        sigmoid(1, 3)
-        scores(2, 2)
+        sigmoids(1, 2)
         quantize_q(2)
-        quantize_w(1, 0, 2)
-        values(1, 0, 2)
-        weigh(1, 2, 4)
-        sigmoid(2, 0)
-        sigmoid(2, 1)
-        scores(3, 0)
-        pack_v(scopy, 2)
+        weigh(1, 2, H)
+
+        sigmoids(2, 0)
+        pack_v(on_scalar, 2)
         weigh(2, 0, 2)
-        quantize_w(1, 2, 4)
-        sigmoid(2, 2)
-        sigmoid(2, 3)
-        scores(3, 2)
-        pack_v(scopy, 3)
-        quantize_w(2, 0, 2)
-        values(2, 0, 2)
-        weigh(2, 2, 4)
-        sigmoid(3, 0)
-        sigmoid(3, 1)
+        quantize_w(1, 0, H)
+        sigmoids(2, 2)
+        pack_v(on_scalar, 3)
+        values(0, 0, 2)
+        values(1, 0, 2)
+        weigh(2, 2, H)
+
+        sigmoids(3, 0)
+        gates(0, 0, H)
         gates(1, 0, 2)
-        gates(0, 0, 4)
-        quantize_v(2, 4)
-        values(0, 2, 4)
-        values(1, 2, 4)
-        quantize_w(2, 2, 4)
-        values(2, 2, 4)
+        quantize_v(2, H)
+        values(0, 2, H)
+        values(1, 2, H)
+        quantize_w(2, 0, H)
+        values(2, 0, H)
         weigh(3, 0, 2)
-        sigmoid(3, 2)
-        sigmoid(3, 3)
-        gates(2, 0, 4)
-        gates(1, 2, 4)
+        sigmoids(3, 2)
+        gates(1, 2, H)
+        gates(2, 0, H)
+
         finish(1, 0, 2)
         quantize_w(3, 0, 2)
         values(3, 0, 2)
-        finish(0, 0, 4)
-        weigh(3, 2, 4)
+        finish(0, 0, H)
+        weigh(3, 2, H)
         finish(2, 0, 2)
-        quantize_w(3, 2, 4)
-        values(3, 2, 4)
-        finish(1, 2, 4)
-        finish(2, 2, 4)
+        quantize_w(3, 2, H)
+        values(3, 2, H)
+        finish(1, 2, H)
+        finish(2, 2, H)

from contextlib import ExitStack

import concourse.mybir as mybir

H, D, NQ, N, E = 4, 128, 512, 512, 128
FLOPS = 2 * H * N * NQ * D + 2 * H * NQ * N * E

F32 = mybir.dt.float32
BF16 = mybir.dt.bfloat16
U32 = mybir.dt.uint32
U8 = mybir.dt.uint8
FP8X4 = mybir.dt.float8_e4m3fn_x4
SIGMOID = mybir.ActivationFunctionType.Sigmoid
MULT = mybir.AluOpType.mult

P = 128
PACK = 4
ROWS = D // PACK
QB = 128
UNIT = QB * PACK
LINE = 4

GROUPS = ((0, 1), (128, 2), (384, 1))
ROUNDS = tuple((g, x) for g, (q0, m) in enumerate(GROUPS) for x in range(m))
V_LOADS = ((0, 1), (1, 2), (2, 4))
K_SPLIT = 56
Q_SPLIT = 40


def tile_rows_sigmoid_gate_kernel(tc, qT, kT, t, v, og, out):
    nc = tc.nc
    with ExitStack() as ctx:
        sb = ctx.enter_context(tc.tile_pool(name="sb", bufs=1))
        ps = ctx.enter_context(tc.psum_pool(name="ps", bufs=1))
        ctx.enter_context(tc.manual_schedule())

        def tile(name, shape, dtype):
            return sb.tile(shape, dtype, name=name, align_bytes=64)

        def by_group(name, shape, dtype):
            return [tile("%s%d" % (name, g), shape(m), dtype) for g, (q0, m) in enumerate(GROUPS)]

        def by_round(name, shape, dtype):
            return [tile("%s%d" % (name, n), shape, dtype) for n in range(len(ROUNDS))]

        k_raw = tile("k_raw", [P, PACK, N], F32)
        q_raw = by_group("q_raw", lambda m: [P, PACK, m * QB], F32)
        v_raw = [tile("v_raw%d" % h0, [P, h1 - h0, PACK, E], F32) for h0, h1 in V_LOADS]
        og_raw = by_group("og_raw", lambda m: [P, H * m * E], F32)
        t_sb = tile("t_sb", [P, PACK], F32)
        warm_in = tile("warm_in", [P, 8], F32)
        warm_out = tile("warm_out", [P, 8], F32)

        k_bf = tile("k_bf", [P, N * PACK], BF16)
        k_codes = tile("k_codes", [P, N], U32)
        k_scales = tile("k_scales", [P, N], U8)
        q_bf = by_group("q_bf", lambda m: [P, m * UNIT], BF16)
        q_codes = by_group("q_codes", lambda m: [P, m * QB], U32)
        q_scales = by_group("q_scales", lambda m: [P, m * QB], U8)
        v_bf = tile("v_bf", [P, H * E * PACK], BF16)
        v_codes = tile("v_codes", [P, H * E], U32)
        v_scales = tile("v_scales", [P, H * E], U8)
        p_sb = by_round("p_sb", [P, H * UNIT], F32)
        w_bf = by_round("w_bf", [P, H * UNIT], BF16)
        w_codes = by_round("w_codes", [P, H * QB], U32)
        w_scales = by_round("w_scales", [P, H * QB], U8)
        gate = by_group("gate", lambda m: [P, H * m * E], F32)
        res = by_group("res", lambda m: [P, H * m * E], F32)
        s_bank = [ps.tile([P, UNIT], F32, name="s_bank%d" % h) for h in range(H)]
        y_bank = [ps.tile([P, 4 * E], F32, name="y_bank%d" % b) for b in range(4)]

        q_rows = qT.rearrange("h (p j) n -> (h p) j n", j=PACK)
        k_rows = kT.rearrange("h (p j) n -> (h p) j n", j=PACK)
        v_rows = v.rearrange("h (p j) e -> p h j e", j=PACK)

        def query_rows(x, g):
            q0, m = GROUPS[g]
            return x[:, q0 : q0 + m * QB, :].rearrange("h (p x) e -> p h (x e)", x=m)

        def load_q(g):
            q0, m = GROUPS[g]
            nc.sync.dma_start(out=q_raw[g][:], in_=q_rows[:, :, q0 : q0 + m * QB])

        def load_v(c):
            h0, h1 = V_LOADS[c]
            nc.sync.dma_start(out=v_raw[c][:], in_=v_rows[:, h0:h1, :, :])

        nc.sync.dma_start(out=k_raw[:], in_=k_rows)
        load_q(0)
        load_q(1)
        load_v(0)
        nc.sync.dma_start(out=t_sb[:], in_=t.rearrange("(p j) o -> p (j o)", j=PACK))
        load_v(1)
        load_q(2)
        load_v(2)
        for g in range(len(GROUPS)):
            nc.sync.dma_start(out=og_raw[g][:].rearrange("p (h f) -> p h f", h=H), in_=query_rows(og, g))

        nc.gpsimd.memset(warm_in[:], 0.0)
        nc.scalar.activation(out=warm_out[:], in_=warm_in[:], func=SIGMOID)

        def quantize(codes, scales, values, w0, w1):
            nc.vector.quantize_mx(
                out=codes[:, w0:w1].bitcast(FP8X4), scales=scales[:, w0:w1], in_=values[:, PACK * w0 : PACK * w1]
            )

        def pack_k(copy, r0, s0, s1):
            copy(
                out=k_bf[:].rearrange("p (r s j) -> p s j r", r=PACK, j=PACK)[:, s0:s1, :, r0 : r0 + 2],
                in_=k_raw[:].rearrange("p j (s r) -> p s j r", r=PACK)[:, s0:s1, :, r0 : r0 + 2],
            )

        def pack_q(copy, g, c0=0, c1=None):
            m = GROUPS[g][1]
            copy(
                out=q_bf[g][:].rearrange("p (x c i j) -> p c j i x", x=m, i=LINE // m, j=PACK)[:, c0:c1],
                in_=q_raw[g][:].rearrange("p j (c i x) -> p c j i x", x=m, i=LINE // m)[:, c0:c1],
            )

        def pack_v(copy, h):
            c = min(h, len(V_LOADS) - 1)
            copy(
                out=v_bf[:, h * UNIT : (h + 1) * UNIT].rearrange("p (c i j) -> p c j i", i=LINE, j=PACK),
                in_=v_raw[c][:, h - V_LOADS[c][0]].rearrange("p j (c i) -> p c j i", i=LINE),
            )

        def quantize_q(g):
            quantize(q_codes[g], q_scales[g], q_bf[g], 0, GROUPS[g][1] * QB)

        def quantize_v(h0, h1):
            quantize(v_codes, v_scales, v_bf, h0 * E, h1 * E)

        def scores(n, h0):
            g, x = ROUNDS[n]
            queries = slice(QB * x, QB * (x + 1))
            for r in range(PACK):
                tokens = slice(r * P, (r + 1) * P)
                for h in (h0 + 1, h0):
                    rows = slice(ROWS * h, ROWS * (h + 1))
                    nc.tensor.matmul_mx(
                        out=s_bank[h][:, r * QB : (r + 1) * QB],
                        lhsT=k_codes[rows, tokens].bitcast(FP8X4),
                        lhsT_scale=k_scales[rows, tokens],
                        rhs=q_codes[g][rows, queries].bitcast(FP8X4),
                        rhs_scale=q_scales[g][rows, queries],
                        start=True,
                        stop=True,
                    )

        def sigmoids(n, h0):
            for h in (h0, h0 + 1):
                nc.scalar.activation(
                    out=p_sb[n][:, h * UNIT : (h + 1) * UNIT].rearrange("p (q r) -> p q r", r=PACK),
                    in_=s_bank[h][:].rearrange("p (r q) -> p q r", r=PACK),
                    func=SIGMOID,
                )
            if n + 1 < len(ROUNDS):
                scores(n + 1, h0)

        def weigh(n, h0, h1):
            cols = slice(h0 * UNIT, h1 * UNIT)
            nc.vector.tensor_tensor(
                out=w_bf[n][:, cols].rearrange("p (q r) -> p q r", r=PACK),
                in0=p_sb[n][:, cols].rearrange("p (q r) -> p q r", r=PACK),
                in1=t_sb[:, 0:PACK].unsqueeze(1).to_broadcast([P, (h1 - h0) * QB, PACK]),
                op=MULT,
            )

        def quantize_w(n, h0, h1):
            quantize(w_codes[n], w_scales[n], w_bf[n], h0 * QB, h1 * QB)

        def y_place(n, h):
            g, x = ROUNDS[n]
            if g == 0:
                return 0, h * E
            if g == 1:
                return 1 + h // 2, ((h % 2) * 2 + x) * E
            return (3 if h < 2 else 0), (h % 2) * E

        def values(n, h0, h1):
            for h in range(h0, h1):
                b, c0 = y_place(n, h)
                nc.tensor.matmul_mx(
                    out=y_bank[b][:, c0 : c0 + E],
                    lhsT=w_codes[n][:, h * QB : (h + 1) * QB].bitcast(FP8X4),
                    lhsT_scale=w_scales[n][:, h * QB : (h + 1) * QB],
                    rhs=v_codes[:, h * E : (h + 1) * E].bitcast(FP8X4),
                    rhs_scale=v_scales[:, h * E : (h + 1) * E],
                    start=True,
                    stop=True,
                )

        def gates(g, h0, h1):
            cols = slice(h0 * GROUPS[g][1] * E, h1 * GROUPS[g][1] * E)
            nc.scalar.activation(out=gate[g][:, cols], in_=og_raw[g][:, cols], func=SIGMOID)

        def finish(g, h0, h1):
            m = GROUPS[g][1]
            b, c0 = y_place(ROUNDS.index((g, 0)), h0)
            cols = slice(h0 * m * E, h1 * m * E)
            nc.vector.scalar_tensor_tensor(
                out=res[g][:, cols],
                in0=y_bank[b][:, c0 : c0 + (h1 - h0) * m * E],
                scalar=1.0 / 16.0,
                in1=gate[g][:, cols],
                op0=MULT,
                op1=MULT,
            )
            nc.sync.dma_start(
                out=query_rows(out, g)[:, h0:h1, :],
                in_=res[g][:, cols].rearrange("p (h f) -> p h f", f=m * E),
            )

        on_vector, on_scalar = nc.vector.tensor_copy, nc.scalar.copy

        pack_k(on_vector, 0, 0, P)
        pack_k(on_vector, 2, 0, K_SPLIT)
        pack_k(on_scalar, 2, K_SPLIT, P)
        pack_q(on_scalar, 0)
        quantize(k_codes, k_scales, k_bf, 0, N // 2)
        quantize(k_codes, k_scales, k_bf, N // 2, N)
        quantize_q(0)
        scores(0, 0)
        scores(0, 2)
        pack_q(on_vector, 1, 0, Q_SPLIT)
        pack_q(on_scalar, 1, Q_SPLIT)
        pack_v(on_vector, 0)
        quantize_q(1)
        pack_v(on_vector, 1)


        for h0 in (0, 2):
            sigmoids(0, h0)
            weigh(0, h0, h0 + 1)
            weigh(0, h0 + 1, h0 + 2)

        sigmoids(1, 0)
        pack_q(on_scalar, 2)
        quantize_v(0, 2)
        quantize_w(0, 0, H)
        weigh(1, 0, 2)
        sigmoids(1, 2)
        quantize_q(2)
        weigh(1, 2, H)

        sigmoids(2, 0)
        pack_v(on_scalar, 2)
        weigh(2, 0, 2)
        quantize_w(1, 0, H)
        sigmoids(2, 2)
        pack_v(on_scalar, 3)
        values(0, 0, 2)
        values(1, 0, 2)
        weigh(2, 2, H)

        sigmoids(3, 0)
        gates(0, 0, H)
        gates(1, 0, 2)
        quantize_v(2, H)
        values(0, 2, H)
        values(1, 2, H)
        quantize_w(2, 0, H)
        values(2, 0, H)
        weigh(3, 0, 2)
        sigmoids(3, 2)
        gates(1, 2, H)
        gates(2, 0, H)

        finish(1, 0, 2)
        quantize_w(3, 0, 2)
        values(3, 0, 2)
        finish(0, 0, H)
        weigh(3, 2, H)
        finish(2, 0, 2)
        quantize_w(3, 2, H)
        values(3, 2, H)
        finish(1, 2, H)
        finish(2, 2, H)
